import numpy as np
import ml_dtypes


def mxq(x, axis, fmt="e4m3"):
    dtype, down = {"e4m3": (ml_dtypes.float8_e4m3fn, 7), "e5m2": (ml_dtypes.float8_e5m2, 14)}[fmt]
    v = np.moveaxis(np.asarray(x, np.float32).astype(ml_dtypes.bfloat16).astype(np.float64), axis, -1)
    blocks = v.reshape(v.shape[:-1] + (-1, 32))
    amax = np.abs(blocks).max(-1, keepdims=True)
    byte = np.maximum(np.where(amax > 0, np.frexp(amax)[1] - 1 + 127, 0) - down, 1)
    scale = np.exp2(byte - 127.0)
    codes = (blocks / scale).astype(np.float32).astype(dtype).astype(np.float64)
    return np.moveaxis((codes * scale).reshape(v.shape), -1, axis)


WIDE = False


def mx_kscale(k):
    if not WIDE:
        return np.ones(k)
    levels = np.array([10, -10, 5, -5, 0])
    if k % 512:
        return np.exp2(np.random.permutation(np.resize(levels, k // 32))).repeat(32)
    a = np.empty((k // 512, 16))
    for p in range(k // 512):
        a[p, :8] = np.random.permutation(np.resize(levels, 8))
        for g in range(8):
            far = levels[np.abs(levels - a[p, g]) >= 10]
            a[p, g + 8] = far[np.random.randint(len(far))]
    return np.exp2(a.ravel()).repeat(32)


def f64(x):
    return np.asarray(x).astype(np.float64)


def split(x):
    m, e = np.frexp(f64(x))
    hi = np.ldexp(np.trunc(16.0 * m) / 16.0, e)
    return hi, f64(x) - hi


K, M, T = 1536, 1024, 1024


def setup_inputs():
    n = np.random.standard_normal
    s = mx_kscale(K)[:, None]
    return {
        "w": (n((K, M)) / np.sqrt(K) / s).astype(np.float32),
        "x": (n((K, T)) * s).astype(np.float32),
        "r": (n((1024, 1024))).astype(np.float32),
    }


def reference(w, x, r):
    w_hi, w_lo = split(w)
    w_hi_, w_lo_ = mxq(w_hi, 0, "e4m3"), mxq(w_lo, 0, "e4m3")
    x_ = mxq(f64(x), 0, "e4m3")
    y = x_.T @ w_hi_ + x_.T @ w_lo_
    return f64(r) + y

@@ -1,0 +1,302 @@
+from contextlib import ExitStack
+import concourse.mybir as mybir
+K, M, T = 1536, 1024, 1024
+FLOPS = 2 * 2 * K * M * T
+F32 = mybir.dt.float32
+BF16 = mybir.dt.bfloat16
+I32 = mybir.dt.int32
+U32 = mybir.dt.uint32
+U8 = mybir.dt.uint8
+FP8X4 = mybir.dt.float8_e4m3fn_x4
+ALU = mybir.AluOpType
+MASK = -0x000F0010
+LOADS = [('W', 0, 0, 0),
+    ('W', 0, 0, 1),
+    ('W', 1, 0, None),
+    ('W', 0, 1, None),
+    ('W', 2, 0, None),
+    ('X', 0, 0, None),
+    ('X', 1, 0, None),
+    ('W', 1, 1, None),
+    ('X', 2, 0, None),
+    ('X', 1, 1, None),
+    ('R', 0, 0, None),
+    ('X', 2, 1, None),
+    ('X', 0, 1, None),
+    ('W', 2, 1, None),
+    ('R', 0, 1, None),
+    ('R', 1, 0, None),
+    ('R', 1, 1, None)]
+SEQ = [('tr', 0, 0, 0, 'v'),
+    ('and', 0, 0, 0),
+    ('tr', 0, 0, 1, 's'),
+    ('sub', 0, 0, 0),
+    ('and', 0, 0, 1),
+    ('qh', 0, 0),
+    ('tr', 1, 0, 0, 's'),
+    ('sub', 0, 0, 1),
+    ('tr', 1, 0, 1, 's'),
+    ('and', 1, 0, 0),
+    ('ql', 0, 0),
+    ('sub', 1, 0, 0),
+    ('tr', 0, 1, 0, 's'),
+    ('and', 1, 0, 1),
+    ('tr', 0, 1, 1, 's'),
+    ('and', 0, 1, 0),
+    ('qh', 1, 0),
+    ('sub', 1, 0, 1),
+    ('tr', 2, 0, 0, 's'),
+    ('and', 0, 1, 1),
+    ('ql', 1, 0),
+    ('tr', 2, 0, 1, 's'),
+    ('qh', 0, 1),
+    ('sub', 0, 1, 0),
+    ('cast', 0, 0, 's'),
+    ('sub', 0, 1, 1),
+    ('and', 2, 0, 0),
+    ('ql', 0, 1),
+    ('cast', 1, 0, 's'),
+    ('qx', 0, 0),
+    ('sub', 2, 0, 0),
+    ('mm', 0, 0, 0, 0, True, False),
+    ('mm', 0, 0, 0, 1, False, False),
+    ('mm', 0, 1, 0, 0, True, False),
+    ('mm', 0, 1, 0, 1, False, False),
+    ('and', 2, 0, 1),
+    ('mm', 0, 2, 0, 0, True, False),
+    ('mm', 0, 2, 0, 1, False, False),
+    ('tr', 1, 1, 0, 's'),
+    ('qh', 2, 0),
+    ('mm', 0, 3, 0, 0, True, False),
+    ('mm', 0, 3, 0, 1, False, False),
+    ('qx', 1, 0),
+    ('mm', 1, 0, 0, 0, True, False),
+    ('mm', 1, 0, 0, 1, False, False),
+    ('sub', 2, 0, 1),
+    ('tr', 1, 1, 1, 's'),
+    ('mm', 1, 1, 0, 0, True, False),
+    ('mm', 0, 0, 1, 0, False, False),
+    ('mm', 0, 0, 1, 1, False, False),
+    ('mm', 0, 1, 1, 0, False, False),
+    ('and', 1, 1, 0),
+    ('mm', 0, 1, 1, 1, False, False),
+    ('cast', 2, 0, 's'),
+    ('ql', 2, 0),
+    ('mm', 0, 2, 1, 0, False, False),
+    ('mm', 0, 2, 1, 1, False, False),
+    ('and', 1, 1, 1),
+    ('mm', 0, 3, 1, 0, False, False),
+    ('sub', 1, 1, 0),
+    ('mm', 0, 3, 1, 1, False, False),
+    ('mm', 1, 1, 0, 1, False, False),
+    ('mm', 1, 2, 0, 0, True, False),
+    ('mm', 1, 2, 0, 1, False, False),
+    ('qh', 1, 1),
+    ('mm', 1, 3, 0, 0, True, False),
+    ('mm', 1, 3, 0, 1, False, False),
+    ('cast', 1, 1, 's'),
+    ('sub', 1, 1, 1),
+    ('mm', 1, 0, 1, 0, False, False),
+    ('mm', 1, 1, 1, 0, False, False),
+    ('mm', 1, 2, 1, 0, False, False),
+    ('mm', 1, 3, 1, 0, False, False),
+    ('qx', 2, 0),
+    ('ql', 1, 1),
+    ('mm', 0, 0, 2, 0, False, False),
+    ('mm', 0, 0, 2, 1, False, True),
+    ('mm', 0, 1, 2, 0, False, False),
+    ('cast', 2, 1, 's'),
+    ('qx', 1, 1),
+    ('mm', 0, 1, 2, 1, False, True),
+    ('mm', 0, 2, 2, 0, False, False),
+    ('epi', 0, 0),
+    ('mm', 0, 2, 2, 1, False, True),
+    ('mm', 0, 3, 2, 0, False, False),
+    ('epi', 0, 1),
+    ('mm', 0, 3, 2, 1, False, True),
+    ('mm', 1, 0, 1, 1, False, False),
+    ('epi', 0, 2),
+    ('mm', 1, 1, 1, 1, False, False),
+    ('mm', 1, 2, 1, 1, False, False),
+    ('epi', 0, 3),
+    ('mm', 1, 3, 1, 1, False, False),
+    ('cast', 0, 1, 's'),
+    ('mm', 0, 4, 1, 0, True, False),
+    ('qx', 2, 1),
+    ('mm', 0, 4, 1, 1, False, False),
+    ('mm', 0, 5, 1, 0, True, False),
+    ('mm', 0, 5, 1, 1, False, False),
+    ('mm', 0, 4, 2, 0, False, False),
+    ('mm', 0, 4, 2, 1, False, False),
+    ('mm', 0, 5, 2, 0, False, False),
+    ('mm', 0, 5, 2, 1, False, False),
+    ('mm', 0, 6, 1, 0, True, False),
+    ('tr', 2, 1, 0, 's'),
+    ('qx', 0, 1),
+    ('mm', 0, 6, 1, 1, False, False),
+    ('mm', 0, 6, 2, 0, False, False),
+    ('mm', 0, 6, 2, 1, False, False),
+    ('mm', 0, 4, 0, 0, False, False),
+    ('tr', 2, 1, 1, 's'),
+    ('mm', 0, 4, 0, 1, False, True),
+    ('and', 2, 1, 0),
+    ('mm', 0, 5, 0, 0, False, False),
+    ('mm', 0, 5, 0, 1, False, True),
+    ('epi', 0, 4),
+    ('mm', 0, 6, 0, 0, False, False),
+    ('mm', 0, 6, 0, 1, False, True),
+    ('sub', 2, 1, 0),
+    ('mm', 0, 7, 0, 0, True, False),
+    ('mm', 0, 7, 0, 1, False, False),
+    ('mm', 0, 7, 1, 0, False, False),
+    ('and', 2, 1, 1),
+    ('mm', 0, 7, 1, 1, False, False),
+    ('epi', 0, 5),
+    ('mm', 0, 7, 2, 0, False, False),
+    ('mm', 0, 7, 2, 1, False, True),
+    ('mm', 1, 4, 0, 0, True, False),
+    ('qh', 2, 1),
+    ('mm', 1, 4, 0, 1, False, False),
+    ('mm', 1, 4, 1, 0, False, False),
+    ('sub', 2, 1, 1),
+    ('mm', 1, 0, 2, 0, False, False),
+    ('mm', 1, 1, 2, 0, False, False),
+    ('mm', 1, 2, 2, 0, False, False),
+    ('mm', 1, 3, 2, 0, False, False),
+    ('epi', 0, 6),
+    ('mm', 1, 4, 1, 1, False, False),
+    ('mm', 1, 4, 2, 0, False, False),
+    ('ql', 2, 1),
+    ('mm', 1, 5, 0, 0, True, False),
+    ('mm', 1, 5, 0, 1, False, False),
+    ('epi', 0, 7),
+    ('mm', 1, 0, 2, 1, False, True),
+    ('mm', 1, 1, 2, 1, False, True),
+    ('mm', 1, 2, 2, 1, False, True),
+    ('epi', 1, 0),
+    ('mm', 1, 3, 2, 1, False, True),
+    ('mm', 1, 4, 2, 1, False, True),
+    ('epi', 1, 1),
+    ('mm', 1, 5, 1, 0, False, False),
+    ('mm', 1, 5, 1, 1, False, False),
+    ('epi', 1, 2),
+    ('mm', 1, 5, 2, 0, False, False),
+    ('mm', 1, 5, 2, 1, False, True),
+    ('epi', 1, 3),
+    ('mm', 1, 6, 0, 0, True, False),
+    ('mm', 1, 6, 0, 1, False, False),
+    ('epi', 1, 4),
+    ('mm', 1, 6, 1, 0, False, False),
+    ('mm', 1, 6, 1, 1, False, False),
+    ('epi', 1, 5),
+    ('mm', 1, 6, 2, 0, False, False),
+    ('mm', 1, 6, 2, 1, False, True),
+    ('mm', 1, 7, 0, 0, True, False),
+    ('mm', 1, 7, 0, 1, False, False),
+    ('epi', 1, 6),
+    ('mm', 1, 7, 1, 0, False, False),
+    ('mm', 1, 7, 1, 1, False, False),
+    ('mm', 1, 7, 2, 0, False, False),
+    ('mm', 1, 7, 2, 1, False, True),
+    ('epi', 1, 7)]
+
+
+def tile_mix_hilo_tm_res_kernel(tc, w, x, r, out):
+    nc = tc.nc
+    with ExitStack() as ctx:
+        ctx.enter_context(tc.manual_schedule())
+        raw = ctx.enter_context(tc.tile_pool(name="raw", bufs=1))
+        keep = ctx.enter_context(tc.tile_pool(name="keep", bufs=1))
+        stage = ctx.enter_context(tc.tile_pool(name="stage", bufs=3))
+        psum = ctx.enter_context(tc.psum_pool(name="psum", bufs=8))
+        wt = {}
+        xt = {}
+        rt = {}
+        for (kind, a, b, piece) in LOADS:
+            if kind == "W":
+                if (a, b) not in wt:
+                    tw = raw.tile([128, 4, 512], F32, name="w%d%d" % (a, b), align_bytes=64)
+                    wt[a, b] = tw
+                src = w[a * 512:(a + 1) * 512, b * 512:(b + 1) * 512].rearrange("(p j) n -> p j n", j=4)
+                if piece is None:
+                    nc.sync.dma_start(out=wt[a, b][:], in_=src)
+                else:
+                    s = slice(piece * 256, piece * 256 + 256)
+                    nc.sync.dma_start(out=wt[a, b][:, :, s], in_=src[:, :, s])
+            elif kind == "X":
+                tx = raw.tile([128, 4, 512], F32, name="x%d%d" % (a, b), align_bytes=64)
+                xt[a, b] = tx
+                nc.sync.dma_start(out=tx[:], in_=x[a * 512:(a + 1) * 512, b * 512:(b + 1) * 512].rearrange("(p j) t -> p j t", j=4))
+            else:
+                tr = raw.tile([128, 4, 512], F32, name="r%d%d" % (a, b), align_bytes=64)
+                rt[a, b] = tr
+                nc.sync.dma_start(out=tr[:], in_=r[b * 512:(b + 1) * 512, a * 512:(a + 1) * 512].rearrange("(m p) n -> p m n", p=128))
+        hi = {}
+        lo = {}
+        xb = {}
+        codes = {}
+        acc = {}
+
+        def il(t, p):
+            return t[:, p * 1024:(p + 1) * 1024].rearrange("p (c i j) -> p c j i", i=4, j=4)
+
+        def quant(key, src):
+            tc_ = keep.tile([128, 512], U32, name="c_%s%d%d" % key, align_bytes=64)
+            ts_ = keep.tile([128, 512], U8, name="s_%s%d%d" % key, align_bytes=64)
+            codes[key] = (tc_, ts_)
+            nc.vector.quantize_mx(out=tc_[:].bitcast(FP8X4), scales=ts_[:], in_=src[:])
+
+        for op in SEQ:
+            k = op[0]
+            if k == "tr":
+                u = op[1:3]
+                p = op[3]
+                if u not in hi:
+                    th = stage.tile([128, 2048], BF16, name="hi", align_bytes=64)
+                    hi[u] = th
+                src = wt[u][:, :, p * 256:p * 256 + 256].bitcast(BF16).rearrange("p j (c i two) -> p c j i two", i=4, two=2)[:, :, :, :, 1]
+                if op[4] == "s":
+                    nc.scalar.copy(out=il(hi[u], p), in_=src)
+                else:
+                    nc.vector.tensor_copy(out=il(hi[u], p), in_=src)
+            elif k == "cast":
+                u = op[1:3]
+                tb = stage.tile([128, 2048], BF16, name="xb", align_bytes=64)
+                xb[u] = tb
+                src = xt[u][:].rearrange("p j (c i) -> p c j i", i=4)
+                dst = tb[:].rearrange("p (c i j) -> p c j i", i=4, j=4)
+                if op[3] == "s":
+                    nc.scalar.copy(out=dst, in_=src)
+                else:
+                    nc.vector.tensor_copy(out=dst, in_=src)
+            elif k == "and":
+                v = hi[op[1:3]][:, op[3] * 1024:(op[3] + 1) * 1024].bitcast(I32)
+                nc.vector.tensor_scalar(out=v, in0=v, scalar1=MASK, scalar2=None, op0=ALU.bitwise_and)
+            elif k == "sub":
+                u = op[1:3]
+                p = op[3]
+                if u not in lo:
+                    tl = stage.tile([128, 2048], BF16, name="lo", align_bytes=64)
+                    lo[u] = tl
+                src = wt[u][:, :, p * 256:p * 256 + 256].rearrange("p j (c i) -> p c j i", i=4)
+                nc.vector.tensor_tensor(out=il(lo[u], p), in0=src, in1=il(hi[u], p), op=ALU.subtract)
+            elif k == "qh":
+                quant(("h",) + op[1:3], hi[op[1:3]])
+            elif k == "ql":
+                quant(("l",) + op[1:3], lo[op[1:3]])
+            elif k == "qx":
+                quant(("x",) + op[1:3], xb[op[1:3]])
+            elif k == "mm":
+                h, m, c, l, first, last = op[1:]
+                if first:
+                    ta = psum.tile([128, 512], F32, name="acc")
+                    acc[h, m] = ta
+                xc, xs = codes["x", c, m // 4]
+                wc, ws = codes["hl"[l], c, h]
+                s = slice((m % 4) * 128, (m % 4) * 128 + 128)
+                nc.tensor.matmul_mx(out=acc[h, m][:], lhsT=xc[:, s].bitcast(FP8X4), lhsT_scale=xs[:, s], rhs=wc[:].bitcast(FP8X4), rhs_scale=ws[:], start=first, stop=last)
+            else:
+                h, m = op[1:]
+                rr = rt[h, m // 4][:, m % 4, :]
+                nc.vector.tensor_tensor(out=rr, in0=acc[h, m][:], in1=rr, op=ALU.add)
+                nc.sync.dma_start(out=out[m * 128:(m + 1) * 128, h * 512:(h + 1) * 512], in_=rr)

@@ -1,7 +1,10 @@
 from contextlib import ExitStack
+
 import concourse.mybir as mybir
+
 K, M, T = 1536, 1024, 1024
 FLOPS = 2 * 2 * K * M * T
+
 F32 = mybir.dt.float32
 BF16 = mybir.dt.bfloat16
 I32 = mybir.dt.int32
@@ -9,196 +12,27 @@ U32 = mybir.dt.uint32
 U8 = mybir.dt.uint8
 FP8X4 = mybir.dt.float8_e4m3fn_x4
 ALU = mybir.AluOpType
-MASK = -0x000F0010
-LOADS = [('W', 0, 0, 0),
-    ('W', 0, 0, 1),
-    ('W', 1, 0, None),
-    ('W', 0, 1, None),
-    ('W', 2, 0, None),
-    ('X', 0, 0, None),
-    ('X', 1, 0, None),
-    ('W', 1, 1, None),
-    ('X', 2, 0, None),
-    ('X', 1, 1, None),
-    ('R', 0, 0, None),
-    ('X', 2, 1, None),
-    ('X', 0, 1, None),
-    ('W', 2, 1, None),
-    ('R', 0, 1, None),
-    ('R', 1, 0, None),
-    ('R', 1, 1, None)]
-SEQ = [('tr', 0, 0, 0, 'v'),
-    ('and', 0, 0, 0),
-    ('tr', 0, 0, 1, 's'),
-    ('sub', 0, 0, 0),
-    ('and', 0, 0, 1),
-    ('qh', 0, 0),
-    ('tr', 1, 0, 0, 's'),
-    ('sub', 0, 0, 1),
-    ('tr', 1, 0, 1, 's'),
-    ('and', 1, 0, 0),
-    ('ql', 0, 0),
-    ('sub', 1, 0, 0),
-    ('tr', 0, 1, 0, 's'),
-    ('and', 1, 0, 1),
-    ('tr', 0, 1, 1, 's'),
-    ('and', 0, 1, 0),
-    ('qh', 1, 0),
-    ('sub', 1, 0, 1),
-    ('tr', 2, 0, 0, 's'),
-    ('and', 0, 1, 1),
-    ('ql', 1, 0),
-    ('tr', 2, 0, 1, 's'),
-    ('qh', 0, 1),
-    ('sub', 0, 1, 0),
-    ('cast', 0, 0, 's'),
-    ('sub', 0, 1, 1),
-    ('and', 2, 0, 0),
-    ('ql', 0, 1),
-    ('cast', 1, 0, 's'),
-    ('qx', 0, 0),
-    ('sub', 2, 0, 0),
-    ('mm', 0, 0, 0, 0, True, False),
-    ('mm', 0, 0, 0, 1, False, False),
-    ('mm', 0, 1, 0, 0, True, False),
-    ('mm', 0, 1, 0, 1, False, False),
-    ('and', 2, 0, 1),
-    ('mm', 0, 2, 0, 0, True, False),
-    ('mm', 0, 2, 0, 1, False, False),
-    ('tr', 1, 1, 0, 's'),
-    ('qh', 2, 0),
-    ('mm', 0, 3, 0, 0, True, False),
-    ('mm', 0, 3, 0, 1, False, False),
-    ('qx', 1, 0),
-    ('mm', 1, 0, 0, 0, True, False),
-    ('mm', 1, 0, 0, 1, False, False),
-    ('sub', 2, 0, 1),
-    ('tr', 1, 1, 1, 's'),
-    ('mm', 1, 1, 0, 0, True, False),
-    ('mm', 0, 0, 1, 0, False, False),
-    ('mm', 0, 0, 1, 1, False, False),
-    ('mm', 0, 1, 1, 0, False, False),
-    ('and', 1, 1, 0),
-    ('mm', 0, 1, 1, 1, False, False),
-    ('cast', 2, 0, 's'),
-    ('ql', 2, 0),
-    ('mm', 0, 2, 1, 0, False, False),
-    ('mm', 0, 2, 1, 1, False, False),
-    ('and', 1, 1, 1),
-    ('mm', 0, 3, 1, 0, False, False),
-    ('sub', 1, 1, 0),
-    ('mm', 0, 3, 1, 1, False, False),
-    ('mm', 1, 1, 0, 1, False, False),
-    ('mm', 1, 2, 0, 0, True, False),
-    ('mm', 1, 2, 0, 1, False, False),
-    ('qh', 1, 1),
-    ('mm', 1, 3, 0, 0, True, False),
-    ('mm', 1, 3, 0, 1, False, False),
-    ('cast', 1, 1, 's'),
-    ('sub', 1, 1, 1),
-    ('mm', 1, 0, 1, 0, False, False),
-    ('mm', 1, 1, 1, 0, False, False),
-    ('mm', 1, 2, 1, 0, False, False),
-    ('mm', 1, 3, 1, 0, False, False),
-    ('qx', 2, 0),
-    ('ql', 1, 1),
-    ('mm', 0, 0, 2, 0, False, False),
-    ('mm', 0, 0, 2, 1, False, True),
-    ('mm', 0, 1, 2, 0, False, False),
-    ('cast', 2, 1, 's'),
-    ('qx', 1, 1),
-    ('mm', 0, 1, 2, 1, False, True),
-    ('mm', 0, 2, 2, 0, False, False),
-    ('epi', 0, 0),
-    ('mm', 0, 2, 2, 1, False, True),
-    ('mm', 0, 3, 2, 0, False, False),
-    ('epi', 0, 1),
-    ('mm', 0, 3, 2, 1, False, True),
-    ('mm', 1, 0, 1, 1, False, False),
-    ('epi', 0, 2),
-    ('mm', 1, 1, 1, 1, False, False),
-    ('mm', 1, 2, 1, 1, False, False),
-    ('epi', 0, 3),
-    ('mm', 1, 3, 1, 1, False, False),
-    ('cast', 0, 1, 's'),
-    ('mm', 0, 4, 1, 0, True, False),
-    ('qx', 2, 1),
-    ('mm', 0, 4, 1, 1, False, False),
-    ('mm', 0, 5, 1, 0, True, False),
-    ('mm', 0, 5, 1, 1, False, False),
-    ('mm', 0, 4, 2, 0, False, False),
-    ('mm', 0, 4, 2, 1, False, False),
-    ('mm', 0, 5, 2, 0, False, False),
-    ('mm', 0, 5, 2, 1, False, False),
-    ('mm', 0, 6, 1, 0, True, False),
-    ('tr', 2, 1, 0, 's'),
-    ('qx', 0, 1),
-    ('mm', 0, 6, 1, 1, False, False),
-    ('mm', 0, 6, 2, 0, False, False),
-    ('mm', 0, 6, 2, 1, False, False),
-    ('mm', 0, 4, 0, 0, False, False),
-    ('tr', 2, 1, 1, 's'),
-    ('mm', 0, 4, 0, 1, False, True),
-    ('and', 2, 1, 0),
-    ('mm', 0, 5, 0, 0, False, False),
-    ('mm', 0, 5, 0, 1, False, True),
-    ('epi', 0, 4),
-    ('mm', 0, 6, 0, 0, False, False),
-    ('mm', 0, 6, 0, 1, False, True),
-    ('sub', 2, 1, 0),
-    ('mm', 0, 7, 0, 0, True, False),
-    ('mm', 0, 7, 0, 1, False, False),
-    ('mm', 0, 7, 1, 0, False, False),
-    ('and', 2, 1, 1),
-    ('mm', 0, 7, 1, 1, False, False),
-    ('epi', 0, 5),
-    ('mm', 0, 7, 2, 0, False, False),
-    ('mm', 0, 7, 2, 1, False, True),
-    ('mm', 1, 4, 0, 0, True, False),
-    ('qh', 2, 1),
-    ('mm', 1, 4, 0, 1, False, False),
-    ('mm', 1, 4, 1, 0, False, False),
-    ('sub', 2, 1, 1),
-    ('mm', 1, 0, 2, 0, False, False),
-    ('mm', 1, 1, 2, 0, False, False),
-    ('mm', 1, 2, 2, 0, False, False),
-    ('mm', 1, 3, 2, 0, False, False),
-    ('epi', 0, 6),
-    ('mm', 1, 4, 1, 1, False, False),
-    ('mm', 1, 4, 2, 0, False, False),
-    ('ql', 2, 1),
-    ('mm', 1, 5, 0, 0, True, False),
-    ('mm', 1, 5, 0, 1, False, False),
-    ('epi', 0, 7),
-    ('mm', 1, 0, 2, 1, False, True),
-    ('mm', 1, 1, 2, 1, False, True),
-    ('mm', 1, 2, 2, 1, False, True),
-    ('epi', 1, 0),
-    ('mm', 1, 3, 2, 1, False, True),
-    ('mm', 1, 4, 2, 1, False, True),
-    ('epi', 1, 1),
-    ('mm', 1, 5, 1, 0, False, False),
-    ('mm', 1, 5, 1, 1, False, False),
-    ('epi', 1, 2),
-    ('mm', 1, 5, 2, 0, False, False),
-    ('mm', 1, 5, 2, 1, False, True),
-    ('epi', 1, 3),
-    ('mm', 1, 6, 0, 0, True, False),
-    ('mm', 1, 6, 0, 1, False, False),
-    ('epi', 1, 4),
-    ('mm', 1, 6, 1, 0, False, False),
-    ('mm', 1, 6, 1, 1, False, False),
-    ('epi', 1, 5),
-    ('mm', 1, 6, 2, 0, False, False),
-    ('mm', 1, 6, 2, 1, False, True),
-    ('mm', 1, 7, 0, 0, True, False),
-    ('mm', 1, 7, 0, 1, False, False),
-    ('epi', 1, 6),
-    ('mm', 1, 7, 1, 0, False, False),
-    ('mm', 1, 7, 1, 1, False, False),
-    ('mm', 1, 7, 2, 0, False, False),
-    ('mm', 1, 7, 2, 1, False, True),
-    ('epi', 1, 7)]
+
+P = 128
+J = 4
+CHUNK = P * J
+CHUNKS = K // CHUNK
+HALF = 512
+PIECE = 256
+RUN = 4
+HI_MASK = -0x000F0010
+
+LOADS = (
+    ("w", 0, 0, 256), ("w", 0, 256, 512), ("w", 1, 0, 1024), ("x", 0, 0, 1024), ("x", 1, 0, 1024),
+    ("w", 2, 0, 512), ("x", 2, 0, 512), ("x", 2, 512, 1024), ("w", 0, 512, 1024), ("r", 0, 0),
+    ("w", 2, 512, 1024), ("r", 0, 1), ("r", 1, 1), ("r", 1, 0),
+)
+PLAN = (
+    "T000* T001 M000 T101 D000 T100 M001 H00 D001 T110* T111 L00 M101 C00 M110 D101 D110 M111 M100 D111 D100 Q00 "
+    "C01 C11 L11 H11 Q01 L10 C10* H10 Q11 Q10 T201 T200 C20 C21 M201 M200 D201 D200 H20 Q20 T011 L20 T010* Q21 "
+    "M010 M011 V06 D010 E00 V07 D011 T211 E03 H01 T210 E02 L01 M211 M210 A06 E01 D210 H21 D211 A07 L21 E05 E04 "
+    "E11 E10 E12 E13 E14 E15 E16 E17"
+)
 
 
 def tile_mix_hilo_tm_res_kernel(tc, w, x, r, out):
@@ -209,94 +43,143 @@ def tile_mix_hilo_tm_res_kernel(tc, w, x, r, out):
         keep = ctx.enter_context(tc.tile_pool(name="keep", bufs=1))
         stage = ctx.enter_context(tc.tile_pool(name="stage", bufs=3))
         psum = ctx.enter_context(tc.psum_pool(name="psum", bufs=8))
-        wt = {}
-        xt = {}
-        rt = {}
-        for (kind, a, b, piece) in LOADS:
-            if kind == "W":
-                if (a, b) not in wt:
-                    tw = raw.tile([128, 4, 512], F32, name="w%d%d" % (a, b), align_bytes=64)
-                    wt[a, b] = tw
-                src = w[a * 512:(a + 1) * 512, b * 512:(b + 1) * 512].rearrange("(p j) n -> p j n", j=4)
-                if piece is None:
-                    nc.sync.dma_start(out=wt[a, b][:], in_=src)
+
+        wf = {}
+        xf = {}
+        rf = {}
+        for load in LOADS:
+            if load[0] == "r":
+                h, g = load[1:]
+                t_r = raw.tile([P, 4, HALF], F32, name="r%d%d" % (h, g), align_bytes=64)
+                src = r[g * HALF : (g + 1) * HALF, h * HALF : (h + 1) * HALF]
+                nc.sync.dma_start(out=t_r[:], in_=src.rearrange("(m p) n -> p m n", p=P))
+                rf[h, g] = t_r
+                continue
+            kind, c, lo, hi = load
+            t_in = raw.tile([P, J, hi - lo], F32, name="%s%d_%d" % (kind, c, lo), align_bytes=64)
+            src = (w if kind == "w" else x)[c * CHUNK : (c + 1) * CHUNK, lo:hi]
+            nc.sync.dma_start(out=t_in[:], in_=src.rearrange("(p j) n -> p j n", j=J))
+            step = PIECE if kind == "w" else HALF
+            for a in range(lo, hi, step):
+                view = t_in[:, :, a - lo : a - lo + step]
+                if kind == "w":
+                    wf[c, a // HALF, a % HALF // PIECE] = view
                 else:
-                    s = slice(piece * 256, piece * 256 + 256)
-                    nc.sync.dma_start(out=wt[a, b][:, :, s], in_=src[:, :, s])
-            elif kind == "X":
-                tx = raw.tile([128, 4, 512], F32, name="x%d%d" % (a, b), align_bytes=64)
-                xt[a, b] = tx
-                nc.sync.dma_start(out=tx[:], in_=x[a * 512:(a + 1) * 512, b * 512:(b + 1) * 512].rearrange("(p j) t -> p j t", j=4))
-            else:
-                tr = raw.tile([128, 4, 512], F32, name="r%d%d" % (a, b), align_bytes=64)
-                rt[a, b] = tr
-                nc.sync.dma_start(out=tr[:], in_=r[b * 512:(b + 1) * 512, a * 512:(a + 1) * 512].rearrange("(m p) n -> p m n", p=128))
-        hi = {}
-        lo = {}
-        xb = {}
-        codes = {}
+                    xf[c, a // HALF] = view
+
+        def grouped(tile, cols):
+            return tile[:, cols.start * J : cols.stop * J].rearrange("p (b i j) -> p b j i", i=RUN, j=J)
+
+        def rows(view):
+            return view.rearrange("p j (b i) -> p b j i", i=RUN)
+
+        def upper_halves(view):
+            return view.bitcast(BF16).rearrange("p j (b i s) -> p b j i s", i=RUN, s=2)[:, :, :, :, 1]
+
+        hi_t = {}
+        lo_t = {}
+        x_t = {}
+        quantised = {}
         acc = {}
+        waiting = {}
+        copied = {}
+        added = set()
+        groups = [(h, m) for h in (0, 1) for m in range(8)]
+        pending = {g: [(c, part) for c in range(CHUNKS) for part in "hl"] for g in groups}
 
-        def il(t, p):
-            return t[:, p * 1024:(p + 1) * 1024].rearrange("p (c i j) -> p c j i", i=4, j=4)
+        def piece_cols(p):
+            return slice(p * PIECE, (p + 1) * PIECE)
 
-        def quant(key, src):
-            tc_ = keep.tile([128, 512], U32, name="c_%s%d%d" % key, align_bytes=64)
-            ts_ = keep.tile([128, 512], U8, name="s_%s%d%d" % key, align_bytes=64)
-            codes[key] = (tc_, ts_)
-            nc.vector.quantize_mx(out=tc_[:].bitcast(FP8X4), scales=ts_[:], in_=src[:])
+        def quantise(key, src):
+            codes = keep.tile([P, HALF], U32, name="codes_%s%d%d" % key, align_bytes=64)
+            scales = keep.tile([P, HALF], U8, name="scales_%s%d%d" % key, align_bytes=64)
+            nc.vector.quantize_mx(out=codes[:].bitcast(FP8X4), scales=scales[:], in_=src[:])
+            quantised[key] = (codes, scales)
 
-        for op in SEQ:
-            k = op[0]
-            if k == "tr":
-                u = op[1:3]
-                p = op[3]
-                if u not in hi:
-                    th = stage.tile([128, 2048], BF16, name="hi", align_bytes=64)
-                    hi[u] = th
-                src = wt[u][:, :, p * 256:p * 256 + 256].bitcast(BF16).rearrange("p j (c i two) -> p c j i two", i=4, two=2)[:, :, :, :, 1]
-                if op[4] == "s":
-                    nc.scalar.copy(out=il(hi[u], p), in_=src)
-                else:
-                    nc.vector.tensor_copy(out=il(hi[u], p), in_=src)
-            elif k == "cast":
-                u = op[1:3]
-                tb = stage.tile([128, 2048], BF16, name="xb", align_bytes=64)
-                xb[u] = tb
-                src = xt[u][:].rearrange("p j (c i) -> p c j i", i=4)
-                dst = tb[:].rearrange("p (c i j) -> p c j i", i=4, j=4)
-                if op[3] == "s":
-                    nc.scalar.copy(out=dst, in_=src)
-                else:
-                    nc.vector.tensor_copy(out=dst, in_=src)
-            elif k == "and":
-                v = hi[op[1:3]][:, op[3] * 1024:(op[3] + 1) * 1024].bitcast(I32)
-                nc.vector.tensor_scalar(out=v, in0=v, scalar1=MASK, scalar2=None, op0=ALU.bitwise_and)
-            elif k == "sub":
-                u = op[1:3]
-                p = op[3]
-                if u not in lo:
-                    tl = stage.tile([128, 2048], BF16, name="lo", align_bytes=64)
-                    lo[u] = tl
-                src = wt[u][:, :, p * 256:p * 256 + 256].rearrange("p j (c i) -> p c j i", i=4)
-                nc.vector.tensor_tensor(out=il(lo[u], p), in0=src, in1=il(hi[u], p), op=ALU.subtract)
-            elif k == "qh":
-                quant(("h",) + op[1:3], hi[op[1:3]])
-            elif k == "ql":
-                quant(("l",) + op[1:3], lo[op[1:3]])
-            elif k == "qx":
-                quant(("x",) + op[1:3], xb[op[1:3]])
-            elif k == "mm":
-                h, m, c, l, first, last = op[1:]
-                if first:
-                    ta = psum.tile([128, 512], F32, name="acc")
-                    acc[h, m] = ta
-                xc, xs = codes["x", c, m // 4]
-                wc, ws = codes["hl"[l], c, h]
-                s = slice((m % 4) * 128, (m % 4) * 128 + 128)
-                nc.tensor.matmul_mx(out=acc[h, m][:], lhsT=xc[:, s].bitcast(FP8X4), lhsT_scale=xs[:, s], rhs=wc[:].bitcast(FP8X4), rhs_scale=ws[:], start=first, stop=last)
+        def multiply():
+            for group in groups:
+                h, m = group
+                ready = [q for q in pending[group] if (q[1], q[0], h) in quantised and ("x", q[0], m // 4) in quantised]
+                if not ready:
+                    continue
+                if group not in acc:
+                    if len(acc) - len(waiting) == 8 or len(acc) != groups.index(group):
+                        continue
+                    bank = psum.tile([P, HALF], F32, name="acc")
+                    acc[group] = bank
+                cols = slice(m % 4 * P, m % 4 * P + P)
+                for c, part in ready:
+                    first = len(pending[group]) == 2 * CHUNKS
+                    pending[group].remove((c, part))
+                    x_codes, x_scales = quantised["x", c, m // 4]
+                    w_codes, w_scales = quantised[part, c, h]
+                    nc.tensor.matmul_mx(
+                        out=acc[group][:],
+                        lhsT=x_codes[:, cols].bitcast(FP8X4),
+                        lhsT_scale=x_scales[:, cols],
+                        rhs=w_codes[:].bitcast(FP8X4),
+                        rhs_scale=w_scales[:],
+                        start=first,
+                        stop=not pending[group],
+                    )
+
+        def finish(h, m, source):
+            r_rows = rf[h, m // 4]
+            row = r_rows[:, m % 4, :]
+            nc.vector.tensor_tensor(out=row, in0=source[:], in1=row, op=ALU.add)
+            added.add((h, m))
+            cols = slice(h * HALF, (h + 1) * HALF)
+            if (h, m // 2) == (1, 3):
+                nc.sync.dma_start(out=out[m * P : (m + 1) * P, cols], in_=row)
+            elif (h, m ^ 1) in added:
+                e = m // 2 * 2
+                dst = out[e * P : (e + 2) * P, cols].rearrange("(m p) n -> p m n", p=P)
+                nc.sync.dma_start(out=dst, in_=r_rows[:, e % 4 : e % 4 + 2, :])
+
+        for token in PLAN.split(" "):
+            name = token.replace("*", "")
+            engine_copy = nc.vector.tensor_copy if "*" in token else nc.scalar.copy
+            op = name[0]
+            a, b = int(name[1]), int(name[2])
+            p = int(name[3:] + "0") // 10
+            if op == "T":
+                if (a, b) not in hi_t:
+                    t_hi = stage.tile([P, HALF * J], BF16, name="hi", align_bytes=64)
+                    hi_t[a, b] = t_hi
+                engine_copy(out=grouped(hi_t[a, b], piece_cols(p)), in_=upper_halves(wf[a, b, p]))
+            elif op == "M":
+                words = hi_t[a, b][:, p * PIECE * J : (p + 1) * PIECE * J].bitcast(I32)
+                nc.vector.tensor_scalar(out=words, in0=words, scalar1=HI_MASK, scalar2=None, op0=ALU.bitwise_and)
+            elif op == "D":
+                if (a, b) not in lo_t:
+                    t_lo = stage.tile([P, HALF * J], BF16, name="lo", align_bytes=64)
+                    lo_t[a, b] = t_lo
+                cols = piece_cols(p)
+                nc.vector.tensor_tensor(
+                    out=grouped(lo_t[a, b], cols), in0=rows(wf[a, b, p]), in1=grouped(hi_t[a, b], cols), op=ALU.subtract
+                )
+            elif op == "C":
+                t_x = stage.tile([P, HALF * J], BF16, name="xb", align_bytes=64)
+                x_t[a, b] = t_x
+                engine_copy(out=grouped(t_x, slice(0, HALF)), in_=rows(xf[a, b]))
+            elif op == "H":
+                quantise(("h", a, b), hi_t[a, b])
+                multiply()
+            elif op == "L":
+                quantise(("l", a, b), lo_t[a, b])
+                multiply()
+            elif op == "Q":
+                quantise(("x", a, b), x_t[a, b])
+                multiply()
+            elif op == "V":
+                t_y = stage.tile([P, HALF], F32, name="y", align_bytes=64)
+                copied[a, b] = t_y
+                nc.scalar.copy(out=t_y[:], in_=acc[a, b][:])
+                waiting[a, b] = True
+                multiply()
+            elif op == "A":
+                finish(a, b, copied[a, b])
             else:
-                h, m = op[1:]
-                rr = rt[h, m // 4][:, m % 4, :]
-                nc.vector.tensor_tensor(out=rr, in0=acc[h, m][:], in1=rr, op=ALU.add)
-                nc.sync.dma_start(out=out[m * 128:(m + 1) * 128, h * 512:(h + 1) * 512], in_=rr)
+                finish(a, b, acc[a, b])
+                waiting[a, b] = True
+                multiply()

@@ -3,7 +3,7 @@ from contextlib import ExitStack
 import concourse.mybir as mybir
 
 K, M, T = 1536, 1024, 1024
-FLOPS = 2 * 2 * K * M * T
+FLOPS = 2 * (2 * K * M * T)
 
 F32 = mybir.dt.float32
 BF16 = mybir.dt.bfloat16
@@ -19,19 +19,26 @@ CHUNK = P * J
 CHUNKS = K // CHUNK
 HALF = 512
 PIECE = 256
+GROUPS_T = T // P
+TILES = HALF // P
+BANKS = 8
 RUN = 4
+
 HI_MASK = -0x000F0010
 
 LOADS = (
     ("w", 0, 0, 256), ("w", 0, 256, 512), ("w", 1, 0, 1024), ("x", 0, 0, 1024), ("x", 1, 0, 1024),
-    ("w", 2, 0, 512), ("x", 2, 0, 512), ("x", 2, 512, 1024), ("w", 0, 512, 1024), ("r", 0, 0),
-    ("w", 2, 512, 1024), ("r", 0, 1), ("r", 1, 1), ("r", 1, 0),
+    ("w", 2, 0, 512), ("x", 2, 0, 512), ("x", 2, 512, 1024), ("w", 0, 512, 1024), ("r", 0, 0, 512),
+    ("w", 2, 512, 1024), ("r", 1, 0, 512), ("r", 0, 512, 1024), ("r", 1, 512, 1024),
 )
+
 PLAN = (
-    "T000* T001 M000 T101 D000 T100 M001 H00 D001 T110* T111 L00 M101 C00 M110 D101 D110 M111 M100 D111 D100 Q00 "
-    "C01 C11 L11 H11 Q01 L10 C10* H10 Q11 Q10 T201 T200 C20 C21 M201 M200 D201 D200 H20 Q20 T011 L20 T010* Q21 "
-    "M010 M011 V06 D010 E00 V07 D011 T211 E03 H01 T210 E02 L01 M211 M210 A06 E01 D210 H21 D211 A07 L21 E05 E04 "
-    "E11 E10 E12 E13 E14 E15 E16 E17"
+    "T000* M000 T001 D000 M001 D001 H00 T101 L00 T111 T110* M110 T100 M101 C00 D110",
+    "C01 C11 M111 D101 T201 M100 D111 D100 Q00 H11 H10 C10* Q01 T200 C20 L11",
+    "Q10 Q11 L10 M201 M200 D201 D200 Q20 C21 T011 L20 H20 T010* Q21 V00 M010",
+    "V01 M011 D010 V03 V02 A01 A03 V06 D011 H01 V07 L01 A02 A00 T211 T210",
+    "M210 M211 D210 H21 D211 A07 L21 A06 V04 A04 E05 E10 E11 E12 E13 E16",
+    "E14 E15 E17",
 )
 
 
@@ -42,144 +49,136 @@ def tile_mix_hilo_tm_res_kernel(tc, w, x, r, out):
         raw = ctx.enter_context(tc.tile_pool(name="raw", bufs=1))
         keep = ctx.enter_context(tc.tile_pool(name="keep", bufs=1))
         stage = ctx.enter_context(tc.tile_pool(name="stage", bufs=3))
-        psum = ctx.enter_context(tc.psum_pool(name="psum", bufs=8))
+        psum = ctx.enter_context(tc.psum_pool(name="psum", bufs=BANKS))
 
-        wf = {}
-        xf = {}
-        rf = {}
-        for load in LOADS:
-            if load[0] == "r":
-                h, g = load[1:]
-                t_r = raw.tile([P, 4, HALF], F32, name="r%d%d" % (h, g), align_bytes=64)
-                src = r[g * HALF : (g + 1) * HALF, h * HALF : (h + 1) * HALF]
-                nc.sync.dma_start(out=t_r[:], in_=src.rearrange("(m p) n -> p m n", p=P))
-                rf[h, g] = t_r
+        w_in = {}
+        x_in = {}
+        r_in = {}
+        for kind, block, lo, hi in LOADS:
+            tile = raw.tile([P, J, hi - lo], F32, name="%s%d_%d" % (kind, block, lo), align_bytes=64)
+            src = {"w": w, "x": x, "r": r}[kind][block * CHUNK : (block + 1) * CHUNK, lo:hi]
+            if kind == "r":
+                nc.sync.dma_start(out=tile[:], in_=src.rearrange("(i p) n -> p i n", p=P))
+                r_in[lo // HALF, block] = tile
                 continue
-            kind, c, lo, hi = load
-            t_in = raw.tile([P, J, hi - lo], F32, name="%s%d_%d" % (kind, c, lo), align_bytes=64)
-            src = (w if kind == "w" else x)[c * CHUNK : (c + 1) * CHUNK, lo:hi]
-            nc.sync.dma_start(out=t_in[:], in_=src.rearrange("(p j) n -> p j n", j=J))
+            nc.sync.dma_start(out=tile[:], in_=src.rearrange("(p j) n -> p j n", j=J))
             step = PIECE if kind == "w" else HALF
-            for a in range(lo, hi, step):
-                view = t_in[:, :, a - lo : a - lo + step]
+            for col in range(lo, hi, step):
+                view = tile[:, :, col - lo : col - lo + step]
                 if kind == "w":
-                    wf[c, a // HALF, a % HALF // PIECE] = view
+                    w_in[block, col // HALF, col % HALF // PIECE] = view
                 else:
-                    xf[c, a // HALF] = view
+                    x_in[block, col // HALF] = view
 
-        def grouped(tile, cols):
-            return tile[:, cols.start * J : cols.stop * J].rearrange("p (b i j) -> p b j i", i=RUN, j=J)
+        def interleaved(tile, lo, hi):
+            return tile[:, lo * J : hi * J].rearrange("p (b i j) -> p b j i", i=RUN, j=J)
 
-        def rows(view):
+        def by_rows(view):
             return view.rearrange("p j (b i) -> p b j i", i=RUN)
 
-        def upper_halves(view):
+        def upper_by_rows(view):
             return view.bitcast(BF16).rearrange("p j (b i s) -> p b j i s", i=RUN, s=2)[:, :, :, :, 1]
 
-        hi_t = {}
-        lo_t = {}
-        x_t = {}
+        hi_units = {}
+        lo_units = {}
+        x_units = {}
         quantised = {}
-        acc = {}
-        waiting = {}
-        copied = {}
-        added = set()
-        groups = [(h, m) for h in (0, 1) for m in range(8)]
-        pending = {g: [(c, part) for c in range(CHUNKS) for part in "hl"] for g in groups}
 
-        def piece_cols(p):
-            return slice(p * PIECE, (p + 1) * PIECE)
-
-        def quantise(key, src):
+        def quantise(key, unit):
             codes = keep.tile([P, HALF], U32, name="codes_%s%d%d" % key, align_bytes=64)
             scales = keep.tile([P, HALF], U8, name="scales_%s%d%d" % key, align_bytes=64)
-            nc.vector.quantize_mx(out=codes[:].bitcast(FP8X4), scales=scales[:], in_=src[:])
+            nc.vector.quantize_mx(out=codes[:].bitcast(FP8X4), scales=scales[:], in_=unit[:])
             quantised[key] = (codes, scales)
 
+        groups = [(h, m) for h in (0, 1) for m in range(GROUPS_T)]
+        passes = {group: [(c, part) for c in range(CHUNKS) for part in "HL"] for group in groups}
+        banks = {}
+        emptied = set()
+
         def multiply():
-            for group in groups:
+            for index, group in enumerate(groups):
                 h, m = group
-                ready = [q for q in pending[group] if (q[1], q[0], h) in quantised and ("x", q[0], m // 4) in quantised]
+                ready = [q for q in passes[group] if (q[1], q[0], h) in quantised and ("Q", q[0], m // TILES) in quantised]
                 if not ready:
                     continue
-                if group not in acc:
-                    if len(acc) - len(waiting) == 8 or len(acc) != groups.index(group):
+                if group not in banks:
+                    if len(banks) != index or len(banks) - len(emptied) == BANKS:
                         continue
-                    bank = psum.tile([P, HALF], F32, name="acc")
-                    acc[group] = bank
-                cols = slice(m % 4 * P, m % 4 * P + P)
+                    bank = psum.tile([P, HALF], F32, name="bank")
+                    banks[group] = bank
+                rows = slice(m % TILES * P, (m % TILES + 1) * P)
                 for c, part in ready:
-                    first = len(pending[group]) == 2 * CHUNKS
-                    pending[group].remove((c, part))
-                    x_codes, x_scales = quantised["x", c, m // 4]
+                    start = len(passes[group]) == 2 * CHUNKS
+                    passes[group].remove((c, part))
+                    x_codes, x_scales = quantised["Q", c, m // TILES]
                     w_codes, w_scales = quantised[part, c, h]
                     nc.tensor.matmul_mx(
-                        out=acc[group][:],
-                        lhsT=x_codes[:, cols].bitcast(FP8X4),
-                        lhsT_scale=x_scales[:, cols],
+                        out=banks[group][:],
+                        lhsT=x_codes[:, rows].bitcast(FP8X4),
+                        lhsT_scale=x_scales[:, rows],
                         rhs=w_codes[:].bitcast(FP8X4),
                         rhs_scale=w_scales[:],
-                        start=first,
-                        stop=not pending[group],
+                        start=start,
+                        stop=not passes[group],
                     )
 
-        def finish(h, m, source):
-            r_rows = rf[h, m // 4]
-            row = r_rows[:, m % 4, :]
-            nc.vector.tensor_tensor(out=row, in0=source[:], in1=row, op=ALU.add)
-            added.add((h, m))
-            cols = slice(h * HALF, (h + 1) * HALF)
-            if (h, m // 2) == (1, 3):
-                nc.sync.dma_start(out=out[m * P : (m + 1) * P, cols], in_=row)
-            elif (h, m ^ 1) in added:
-                e = m // 2 * 2
-                dst = out[e * P : (e + 2) * P, cols].rearrange("(m p) n -> p m n", p=P)
-                nc.sync.dma_start(out=dst, in_=r_rows[:, e % 4 : e % 4 + 2, :])
+        finished = set()
 
-        for token in PLAN.split(" "):
-            name = token.replace("*", "")
-            engine_copy = nc.vector.tensor_copy if "*" in token else nc.scalar.copy
-            op = name[0]
-            a, b = int(name[1]), int(name[2])
-            p = int(name[3:] + "0") // 10
-            if op == "T":
-                if (a, b) not in hi_t:
-                    t_hi = stage.tile([P, HALF * J], BF16, name="hi", align_bytes=64)
-                    hi_t[a, b] = t_hi
-                engine_copy(out=grouped(hi_t[a, b], piece_cols(p)), in_=upper_halves(wf[a, b, p]))
-            elif op == "M":
-                words = hi_t[a, b][:, p * PIECE * J : (p + 1) * PIECE * J].bitcast(I32)
+        def add_r_and_store(h, m, sums):
+            tile = r_in[h, m // TILES]
+            block = m % TILES
+            nc.vector.tensor_tensor(out=tile[:, block, :], in0=sums[:], in1=tile[:, block, :], op=ALU.add)
+            finished.add((h, m))
+            cols = slice(h * HALF, (h + 1) * HALF)
+            first = m - m % 2
+            if (h, first) == (1, GROUPS_T - 2):
+                nc.sync.dma_start(out=out[m * P : (m + 1) * P, cols], in_=tile[:, block, :])
+            elif (h, first) in finished and (h, first + 1) in finished:
+                dst = out[first * P : (first + 2) * P, cols].rearrange("(i p) n -> p i n", p=P)
+                nc.sync.dma_start(out=dst, in_=tile[:, first % TILES : first % TILES + 2, :])
+
+        copied = {}
+        for step in " ".join(PLAN).split(" "):
+            copy = nc.vector.tensor_copy if "*" in step else nc.scalar.copy
+            letter = step[0]
+            numbers = [int(digit) for digit in step[1:].replace("*", "")]
+            a, b = numbers[0], numbers[1]
+            if letter in "TMD":
+                piece = numbers[2]
+                lo, hi = piece * PIECE, (piece + 1) * PIECE
+            if letter == "T":
+                if (a, b) not in hi_units:
+                    hi_unit = stage.tile([P, HALF * J], BF16, name="hi_unit", align_bytes=64)
+                    hi_units[a, b] = hi_unit
+                copy(out=interleaved(hi_units[a, b], lo, hi), in_=upper_by_rows(w_in[a, b, piece]))
+            elif letter == "M":
+                words = hi_units[a, b][:, lo * J : hi * J].bitcast(I32)
                 nc.vector.tensor_scalar(out=words, in0=words, scalar1=HI_MASK, scalar2=None, op0=ALU.bitwise_and)
-            elif op == "D":
-                if (a, b) not in lo_t:
-                    t_lo = stage.tile([P, HALF * J], BF16, name="lo", align_bytes=64)
-                    lo_t[a, b] = t_lo
-                cols = piece_cols(p)
+            elif letter == "D":
+                if (a, b) not in lo_units:
+                    lo_unit = stage.tile([P, HALF * J], BF16, name="lo_unit", align_bytes=64)
+                    lo_units[a, b] = lo_unit
                 nc.vector.tensor_tensor(
-                    out=grouped(lo_t[a, b], cols), in0=rows(wf[a, b, p]), in1=grouped(hi_t[a, b], cols), op=ALU.subtract
+                    out=interleaved(lo_units[a, b], lo, hi),
+                    in0=by_rows(w_in[a, b, piece]),
+                    in1=interleaved(hi_units[a, b], lo, hi),
+                    op=ALU.subtract,
                 )
-            elif op == "C":
-                t_x = stage.tile([P, HALF * J], BF16, name="xb", align_bytes=64)
-                x_t[a, b] = t_x
-                engine_copy(out=grouped(t_x, slice(0, HALF)), in_=rows(xf[a, b]))
-            elif op == "H":
-                quantise(("h", a, b), hi_t[a, b])
+            elif letter == "C":
+                x_unit = stage.tile([P, HALF * J], BF16, name="x_unit", align_bytes=64)
+                x_units[a, b] = x_unit
+                copy(out=interleaved(x_unit, 0, HALF), in_=by_rows(x_in[a, b]))
+            elif letter in "HLQ":
+                quantise((letter, a, b), {"H": hi_units, "L": lo_units, "Q": x_units}[letter][a, b])
                 multiply()
-            elif op == "L":
-                quantise(("l", a, b), lo_t[a, b])
-                multiply()
-            elif op == "Q":
-                quantise(("x", a, b), x_t[a, b])
-                multiply()
-            elif op == "V":
-                t_y = stage.tile([P, HALF], F32, name="y", align_bytes=64)
-                copied[a, b] = t_y
-                nc.scalar.copy(out=t_y[:], in_=acc[a, b][:])
-                waiting[a, b] = True
-                multiply()
-            elif op == "A":
-                finish(a, b, copied[a, b])
+            elif letter == "A":
+                add_r_and_store(a, b, copied[a, b])
             else:
-                finish(a, b, acc[a, b])
-                waiting[a, b] = True
+                if letter == "V":
+                    sums = stage.tile([P, HALF], F32, name="sums", align_bytes=64, bufs=7)
+                    copied[a, b] = sums
+                    nc.scalar.copy(out=sums[:], in_=banks[a, b][:])
+                else:
+                    add_r_and_store(a, b, banks[a, b])
+                emptied.add((a, b))
                 multiply()

from contextlib import ExitStack

import concourse.mybir as mybir

K, M, T = 1536, 1024, 1024
FLOPS = 2 * (2 * K * M * T)

F32 = mybir.dt.float32
BF16 = mybir.dt.bfloat16
I32 = mybir.dt.int32
U32 = mybir.dt.uint32
U8 = mybir.dt.uint8
FP8X4 = mybir.dt.float8_e4m3fn_x4
ALU = mybir.AluOpType

P = 128
J = 4
CHUNK = P * J
CHUNKS = K // CHUNK
HALF = 512
PIECE = 256
GROUPS_T = T // P
TILES = HALF // P
BANKS = 8
RUN = 4

HI_MASK = -0x000F0010

LOADS = (
    ("w", 0, 0, 256), ("w", 0, 256, 512), ("w", 1, 0, 1024), ("x", 0, 0, 1024), ("x", 1, 0, 1024),
    ("w", 2, 0, 512), ("x", 2, 0, 512), ("x", 2, 512, 1024), ("w", 0, 512, 1024), ("r", 0, 0, 512),
    ("w", 2, 512, 1024), ("r", 1, 0, 512), ("r", 0, 512, 1024), ("r", 1, 512, 1024),
)

PLAN = (
    "T000* M000 T001 D000 M001 D001 H00 T101 L00 T111 T110* M110 T100 M101 C00 D110",
    "C01 C11 M111 D101 T201 M100 D111 D100 Q00 H11 H10 C10* Q01 T200 C20 L11",
    "Q10 Q11 L10 M201 M200 D201 D200 Q20 C21 T011 L20 H20 T010* Q21 V00 M010",
    "V01 M011 D010 V03 V02 A01 A03 V06 D011 H01 V07 L01 A02 A00 T211 T210",
    "M210 M211 D210 H21 D211 A07 L21 A06 V04 A04 E05 E10 E11 E12 E13 E16",
    "E14 E15 E17",
)


def tile_mix_hilo_tm_res_kernel(tc, w, x, r, out):
    nc = tc.nc
    with ExitStack() as ctx:
        ctx.enter_context(tc.manual_schedule())
        raw = ctx.enter_context(tc.tile_pool(name="raw", bufs=1))
        keep = ctx.enter_context(tc.tile_pool(name="keep", bufs=1))
        stage = ctx.enter_context(tc.tile_pool(name="stage", bufs=3))
        psum = ctx.enter_context(tc.psum_pool(name="psum", bufs=BANKS))

        w_in = {}
        x_in = {}
        r_in = {}
        for kind, block, lo, hi in LOADS:
            tile = raw.tile([P, J, hi - lo], F32, name="%s%d_%d" % (kind, block, lo), align_bytes=64)
            src = {"w": w, "x": x, "r": r}[kind][block * CHUNK : (block + 1) * CHUNK, lo:hi]
            if kind == "r":
                nc.sync.dma_start(out=tile[:], in_=src.rearrange("(i p) n -> p i n", p=P))
                r_in[lo // HALF, block] = tile
                continue
            nc.sync.dma_start(out=tile[:], in_=src.rearrange("(p j) n -> p j n", j=J))
            step = PIECE if kind == "w" else HALF
            for col in range(lo, hi, step):
                view = tile[:, :, col - lo : col - lo + step]
                if kind == "w":
                    w_in[block, col // HALF, col % HALF // PIECE] = view
                else:
                    x_in[block, col // HALF] = view

        def interleaved(tile, lo, hi):
            return tile[:, lo * J : hi * J].rearrange("p (b i j) -> p b j i", i=RUN, j=J)

        def by_rows(view):
            return view.rearrange("p j (b i) -> p b j i", i=RUN)

        def upper_by_rows(view):
            return view.bitcast(BF16).rearrange("p j (b i s) -> p b j i s", i=RUN, s=2)[:, :, :, :, 1]

        hi_units = {}
        lo_units = {}
        x_units = {}
        quantised = {}

        def quantise(key, unit):
            codes = keep.tile([P, HALF], U32, name="codes_%s%d%d" % key, align_bytes=64)
            scales = keep.tile([P, HALF], U8, name="scales_%s%d%d" % key, align_bytes=64)
            nc.vector.quantize_mx(out=codes[:].bitcast(FP8X4), scales=scales[:], in_=unit[:])
            quantised[key] = (codes, scales)

        groups = [(h, m) for h in (0, 1) for m in range(GROUPS_T)]
        passes = {group: [(c, part) for c in range(CHUNKS) for part in "HL"] for group in groups}
        banks = {}
        emptied = set()

        def multiply():
            for index, group in enumerate(groups):
                h, m = group
                ready = [q for q in passes[group] if (q[1], q[0], h) in quantised and ("Q", q[0], m // TILES) in quantised]
                if not ready:
                    continue
                if group not in banks:
                    if len(banks) != index or len(banks) - len(emptied) == BANKS:
                        continue
                    bank = psum.tile([P, HALF], F32, name="bank")
                    banks[group] = bank
                rows = slice(m % TILES * P, (m % TILES + 1) * P)
                for c, part in ready:
                    start = len(passes[group]) == 2 * CHUNKS
                    passes[group].remove((c, part))
                    x_codes, x_scales = quantised["Q", c, m // TILES]
                    w_codes, w_scales = quantised[part, c, h]
                    nc.tensor.matmul_mx(
                        out=banks[group][:],
                        lhsT=x_codes[:, rows].bitcast(FP8X4),
                        lhsT_scale=x_scales[:, rows],
                        rhs=w_codes[:].bitcast(FP8X4),
                        rhs_scale=w_scales[:],
                        start=start,
                        stop=not passes[group],
                    )

        finished = set()

        def add_r_and_store(h, m, sums):
            tile = r_in[h, m // TILES]
            block = m % TILES
            nc.vector.tensor_tensor(out=tile[:, block, :], in0=sums[:], in1=tile[:, block, :], op=ALU.add)
            finished.add((h, m))
            cols = slice(h * HALF, (h + 1) * HALF)
            first = m - m % 2
            if (h, first) == (1, GROUPS_T - 2):
                nc.sync.dma_start(out=out[m * P : (m + 1) * P, cols], in_=tile[:, block, :])
            elif (h, first) in finished and (h, first + 1) in finished:
                dst = out[first * P : (first + 2) * P, cols].rearrange("(i p) n -> p i n", p=P)
                nc.sync.dma_start(out=dst, in_=tile[:, first % TILES : first % TILES + 2, :])

        copied = {}
        for step in " ".join(PLAN).split(" "):
            copy = nc.vector.tensor_copy if "*" in step else nc.scalar.copy
            letter = step[0]
            numbers = [int(digit) for digit in step[1:].replace("*", "")]
            a, b = numbers[0], numbers[1]
            if letter in "TMD":
                piece = numbers[2]
                lo, hi = piece * PIECE, (piece + 1) * PIECE
            if letter == "T":
                if (a, b) not in hi_units:
                    hi_unit = stage.tile([P, HALF * J], BF16, name="hi_unit", align_bytes=64)
                    hi_units[a, b] = hi_unit
                copy(out=interleaved(hi_units[a, b], lo, hi), in_=upper_by_rows(w_in[a, b, piece]))
            elif letter == "M":
                words = hi_units[a, b][:, lo * J : hi * J].bitcast(I32)
                nc.vector.tensor_scalar(out=words, in0=words, scalar1=HI_MASK, scalar2=None, op0=ALU.bitwise_and)
            elif letter == "D":
                if (a, b) not in lo_units:
                    lo_unit = stage.tile([P, HALF * J], BF16, name="lo_unit", align_bytes=64)
                    lo_units[a, b] = lo_unit
                nc.vector.tensor_tensor(
                    out=interleaved(lo_units[a, b], lo, hi),
                    in0=by_rows(w_in[a, b, piece]),
                    in1=interleaved(hi_units[a, b], lo, hi),
                    op=ALU.subtract,
                )
            elif letter == "C":
                x_unit = stage.tile([P, HALF * J], BF16, name="x_unit", align_bytes=64)
                x_units[a, b] = x_unit
                copy(out=interleaved(x_unit, 0, HALF), in_=by_rows(x_in[a, b]))
            elif letter in "HLQ":
                quantise((letter, a, b), {"H": hi_units, "L": lo_units, "Q": x_units}[letter][a, b])
                multiply()
            elif letter == "A":
                add_r_and_store(a, b, copied[a, b])
            else:
                if letter == "V":
                    sums = stage.tile([P, HALF], F32, name="sums", align_bytes=64, bufs=7)
                    copied[a, b] = sums
                    nc.scalar.copy(out=sums[:], in_=banks[a, b][:])
                else:
                    add_r_and_store(a, b, banks[a, b])
                emptied.add((a, b))
                multiply()
